import numpy as np
import ml_dtypes


def mxq(x, axis, fmt="e4m3"):
    dtype, down = {"e4m3": (ml_dtypes.float8_e4m3fn, 7), "e5m2": (ml_dtypes.float8_e5m2, 14)}[fmt]
    v = np.moveaxis(np.asarray(x, np.float32).astype(ml_dtypes.bfloat16).astype(np.float64), axis, -1)
    blocks = v.reshape(v.shape[:-1] + (-1, 32))
    amax = np.abs(blocks).max(-1, keepdims=True)
    byte = np.maximum(np.where(amax > 0, np.frexp(amax)[1] - 1 + 127, 0) - down, 1)
    scale = np.exp2(byte - 127.0)
    codes = (blocks / scale).astype(np.float32).astype(dtype).astype(np.float64)
    return np.moveaxis((codes * scale).reshape(v.shape), -1, axis)


WIDE = False


def mx_kscale(k):
    if not WIDE:
        return np.ones(k)
    levels = np.array([10, -10, 5, -5, 0])
    if k % 512:
        return np.exp2(np.random.permutation(np.resize(levels, k // 32))).repeat(32)
    a = np.empty((k // 512, 16))
    for p in range(k // 512):
        a[p, :8] = np.random.permutation(np.resize(levels, 8))
        for g in range(8):
            far = levels[np.abs(levels - a[p, g]) >= 10]
            a[p, g + 8] = far[np.random.randint(len(far))]
    return np.exp2(a.ravel()).repeat(32)


def f64(x):
    return np.asarray(x).astype(np.float64)


def striped(idx):
    return np.tile(idx.reshape(-1, 16).T, (8, 1)).astype(np.uint16)


def unstriped(offs):
    return offs[:16].T.reshape(-1).astype(np.int64)


def pack_weight(w):
    k, n = w.shape
    w = f64(np.asarray(w, np.float32).astype(ml_dtypes.bfloat16)).reshape(k // 32, 32, n)
    amax = np.abs(w).max(1)
    byte = np.clip(np.where(amax > 0, np.frexp(amax)[1] - 1 + 127 - 7, 1), 1, 254)
    scaled = (w * np.exp2(127.0 - byte)[:, None, :]).reshape(k, n).astype(np.float32)
    words = np.ascontiguousarray(scaled.reshape(k // 512, 128, 4, n).transpose(0, 1, 3, 2)).astype(ml_dtypes.float8_e4m3fn).view(np.uint8)
    return words, np.ascontiguousarray(byte.astype(np.uint8).reshape(k // 512, 16, n))


def unpack_weight(words, scales):
    g, p, n, _ = words.shape
    vals = np.ascontiguousarray(words).view(ml_dtypes.float8_e4m3fn).astype(np.float64) * np.repeat(np.exp2(scales.astype(np.float64) - 127.0), 8, axis=1)[..., None]
    return vals.transpose(0, 1, 3, 2).reshape(g * 512, n)


def relu(v):
    return np.maximum(v, 0.0)


def sigmoid(v):
    return 1.0 / (1.0 + np.exp(-np.maximum(v, -700.0)))


K, T, S, H, Z, W = 512, 2048, 512, 512, 512, 1024
P = 2 ** 7


def setup_inputs():
    n = np.random.standard_normal
    s = mx_kscale(K)[:, None]
    u = mx_kscale(H)
    packed_xT = pack_weight(n((K, T)) * s)
    packed_eT = pack_weight(n((K, W)) * s)
    return {
        "x_words": packed_xT[0],
        "x_scales": packed_xT[1],
        "w1": (n((K, H)) / np.sqrt(K) / s).astype(np.float32),
        "e_words": packed_eT[0],
        "e_scales": packed_eT[1],
        "w2": (n((K, H)) / np.sqrt(K) / s).astype(np.float32),
        "w3": (n((K, H)) / np.sqrt(K) / s).astype(np.float32),
        "unit": (np.random.uniform(0.6, 1.4, (H, 1)) * u[:, None]).astype(np.float32),
        "unit2": (np.random.uniform(0.6, 1.4, (H, 1)) / np.sqrt(H) / u[:, None]).astype(np.float32),
        "bid": (np.tile(np.random.uniform(0.3, 1.5, W), (P, 1))).astype(np.float32),
        "offs": striped(np.random.permutation(T)[:S]),
        "cmp_": striped(np.random.permutation(W)[:Z]),
        "usr": striped(np.random.permutation(S)),
        "run": striped(np.random.permutation(Z)),
    }


def reference(x_words, x_scales, w1, e_words, e_scales, w2, w3, unit, unit2, bid, offs, cmp_, usr, run):
    xq = unpack_weight(x_words, x_scales)[:, unstriped(offs)]
    y = mxq(f64(w1), 0, "e4m3").T @ xq
    yu = y[:, unstriped(usr)]
    ctx1 = y + 0.5 * relu(yu)
    hid = f64(unit) * ctx1
    e_cmp_ = unpack_weight(e_words, e_scales)[:, unstriped(cmp_)]
    ye = mxq(f64(w2), 0, "e4m3").T @ e_cmp_
    yg = mxq(f64(w3), 0, "e4m3").T @ e_cmp_
    ad_ = ye * sigmoid(yg)
    hid2 = f64(unit2) * ad_
    sc = mxq(hid, 0, "e4m3").T @ mxq(hid2, 0, "e4m3")
    val = (np.exp(0.9 * np.tanh(sc))) * (f64(bid)[:1][:, unstriped(cmp_)])
    slot = val.reshape(len(val), -1, 4).max(axis=2)
    short = np.repeat(slot, 4, axis=1) - val
    return np.exp(-1.5 * short) * val[:, unstriped(run)]

@@ -1,0 +1,239 @@
+from contextlib import ExitStack
+
+import concourse.mybir as mybir
+from concourse.masks import make_identity
+
+K, T, W = 512, 2048, 1024
+S = 512
+FLOPS = 4 * 2 * 512 * 512 * 512
+
+F32 = mybir.dt.float32
+BF16 = mybir.dt.bfloat16
+I32 = mybir.dt.int32
+U32 = mybir.dt.uint32
+U16 = mybir.dt.uint16
+U8 = mybir.dt.uint8
+FP8X4 = mybir.dt.float8_e4m3fn_x4
+ALU = mybir.AluOpType
+ACT = mybir.ActivationFunctionType
+
+P = 128
+PACK = 4
+HALF = 256
+LH = HALF // 16
+
+
+def tile_picked_yauctbd_pay_p_kernel(
+    tc, x_words, x_scales, w1, e_words, e_scales, w2, w3, unit, unit2, bid, offs, cmp_, usr, run, out
+):
+    nc = tc.nc
+    with ExitStack() as ctx:
+        keep = ctx.enter_context(tc.tile_pool(name="keep", bufs=1))
+        psum = ctx.enter_context(tc.psum_pool(name="psum", bufs=1))
+
+        def sb(name, shape, dt):
+            return keep.tile(shape, dt, name=name, align_bytes=64)
+
+        offs_t = keep.tile([P, S // 16], U16, name="offs_t")
+        cmp_t = keep.tile([P, S // 16], U16, name="cmp_t")
+        usr_t = keep.tile([P, S // 16], U16, name="usr_t")
+        run_t = keep.tile([P, S // 16], U16, name="run_t")
+
+        x_tab = sb("x_tab", [P, T], I32)
+        e_tab = sb("e_tab", [P, W], I32)
+        xs_tab = sb("xs_tab", [P, T], U8)
+        es_tab = sb("es_tab", [P, W], U8)
+        bid_tab = sb("bid_tab", [P, W], F32)
+        rows = sb("rows", [P, P], F32)
+        ident = sb("ident", [P, P], F32)
+
+        nc.vector.memset(xs_tab[:].bitcast(I32), 0)
+        nc.vector.memset(rows[:], 0.0)
+        nc.vector.memset(es_tab[:].bitcast(I32), 0)
+        make_identity(nc, ident[:])
+
+        def load_scales(eng, tab, scales):
+            for q in range(4):
+                eng.dma_start(out=tab[32 * q : 32 * q + 4, :].bitcast(I32), in_=scales[0, 4 * q : 4 * q + 4, :].bitcast(I32))
+
+        def load_words(tab, words):
+            nc.sync.dma_start(out=tab[:], in_=words[0].rearrange("p n t -> p (n t)").bitcast(I32))
+
+        def load_half(name, w, h):
+            raw = sb(name, [P, PACK, HALF], F32)
+            nc.sync.dma_start(out=raw[:], in_=w.rearrange("(p j) c -> p j c", j=PACK)[:, :, h * HALF : (h + 1) * HALF])
+            return raw
+
+        nc.sync.dma_start(offs_t[:], offs)
+        load_words(x_tab, x_words)
+        load_scales(nc.sync, xs_tab, x_scales)
+        for a, vec in enumerate((unit, unit2)):
+            nc.sync.dma_start(
+                out=rows[4 * a : 4 * a + 4, :].rearrange("t (g r) -> t g r", r=8),
+                in_=vec.rearrange("(g t r) o -> t g (r o)", t=4, r=8),
+            )
+        w1_raw = [load_half("w1_raw%d" % h, w1, h) for h in range(2)]
+        nc.sync.dma_start(cmp_t[:], cmp_)
+        load_words(e_tab, e_words)
+        load_scales(nc.sync, es_tab, e_scales)
+        nc.sync.dma_start(usr_t[:], usr)
+        w2_raw = [load_half("w2_raw%d" % h, w2, h) for h in range(2)]
+        w3_raw = [load_half("w3_raw%d" % h, w3, h) for h in range(2)]
+        nc.sync.dma_start(out=bid_tab[:], in_=bid)
+        nc.sync.dma_start(run_t[:], run)
+
+        def bank(i):
+            return psum.tile([P, S], F32, name="bank%d" % i)
+
+        xq_s = sb("xq_s", [P, S], U8)
+        eq_s = sb("eq_s", [P, S], U8)
+        xq_w = sb("xq_w", [P, S], U32)
+        eq_w = sb("eq_w", [P, S], U32)
+        nc.vector.tensor_copy(xq_w[:], x_tab[:].bitcast(U32).indirect(offs_t[:]))
+        nc.vector.tensor_copy(xq_s[:], xs_tab[:].indirect(offs_t[:]))
+
+        ub = bank(4)
+        nc.tensor.transpose(ub[:, 0:P], rows[:], ident[:])
+        u_abs = sb("u_abs", [P, 4], F32)
+        u_half = sb("u_half", [P, 4], F32)
+        sgn = sb("sgn", [P, 4], F32)
+        h2 = sb("h2", [P, 4], F32)
+        nc.scalar.activation(u_abs[:], ub[:, 0:4], ACT.Abs)
+        nc.scalar.activation(u_half[:], ub[:, 0:4], ACT.Abs, scale=0.5)
+        nc.vector.tensor_scalar(sgn[:], ub[:, 0:4], 0.0, -0.5, ALU.is_ge, ALU.add)
+        nc.vector.tensor_tensor(h2[:], sgn[:], ub[:, 4:8], ALU.mult)
+
+        def cast_half(eng, wb, raw, h):
+            dst = wb[:].rearrange("p (t h g r j) -> p h t g r j", t=4, h=2, g=8, r=8)[:, h]
+            srcv = raw[:].rearrange("p j (g t r) -> p t g r j", t=4, r=8)
+            if eng == "v":
+                nc.vector.tensor_copy(dst, srcv)
+            else:
+                nc.scalar.copy(dst, srcv)
+
+        def quant(name, wb):
+            codes = sb(name + "_c", [P, S], U32)
+            scales = sb(name + "_s", [P, S], U8)
+            nc.vector.quantize_mx(out=codes[:].bitcast(FP8X4), scales=scales[:], in_=wb[:])
+            return codes, scales
+
+        def mm(dst, lq, cols, rw, rs):
+            nc.tensor.matmul_mx(
+                out=dst, lhsT=lq[0][:, cols].bitcast(FP8X4), lhsT_scale=lq[1][:, cols],
+                rhs=rw.bitcast(FP8X4), rhs_scale=rs, start=True, stop=True,
+            )
+
+        w1_b = sb("w1_b", [P, 4 * S], BF16)
+        cast_half("s", w1_b, w1_raw[0], 0)
+        cast_half("v", w1_b, w1_raw[1], 1)
+        w1_q = quant("w1", w1_b)
+
+        y = []
+        relu_y = []
+        for t in range(4):
+            yb = bank(t)
+            mm(yb[:], w1_q, slice(P * t, P * (t + 1)), xq_w[:], xq_s[:])
+            r = sb("relu_y%d" % t, [P, S], F32)
+            nc.scalar.activation(r[:], yb[:], ACT.Relu, scale=u_half[:, t : t + 1])
+            y.append(yb)
+            relu_y.append(r)
+
+        nc.vector.tensor_copy(eq_s[:], es_tab[:].indirect(cmp_t[:]))
+        nc.vector.tensor_copy(eq_w[:], e_tab[:].bitcast(U32).indirect(cmp_t[:]))
+
+        hid_q = []
+
+        def hid_gather(h):
+            got = []
+            for t in range(4):
+                g = sb("ru%d_%d" % (h, t), [P, HALF], F32)
+                nc.scalar.activation(g[:], relu_y[t][:].indirect(usr_t[:, h * LH : (h + 1) * LH]), ACT.Copy)
+                got.append(g)
+            return got
+
+        def hid_finish(h, got):
+            planes = sb("hid_p%d" % h, [P, 4, HALF], BF16)
+            for t in range(4):
+                nc.vector.scalar_tensor_tensor(
+                    planes[:, t, :], y[t][:, h * HALF : (h + 1) * HALF], u_abs[:, t : t + 1], got[t][:], ALU.mult, ALU.add
+                )
+            woven = sb("hid_w%d" % h, [P, HALF, 4], BF16)
+            nc.vector.tensor_copy(woven[:], planes[:].rearrange("p t n -> p n t"))
+            codes = sb("hid_c%d" % h, [P, HALF], U32)
+            scales = sb("hid_s%d" % h, [P, HALF], U8)
+            nc.vector.quantize_mx(out=codes[:].bitcast(FP8X4), scales=scales[:], in_=woven[:].rearrange("p n t -> p (n t)"))
+            hid_q.append((codes, scales))
+
+        got0 = hid_gather(0)
+
+        w2_b = sb("w2_b", [P, 4 * S], BF16)
+        w3_b = sb("w3_b", [P, 4 * S], BF16)
+        cast_half("v", w2_b, w2_raw[0], 0)
+        cast_half("v", w2_b, w2_raw[1], 1)
+        w2_q = quant("w2", w2_b)
+        cast_half("s", w3_b, w3_raw[0], 0)
+        cast_half("v", w3_b, w3_raw[1], 1)
+        w3_q = quant("w3", w3_b)
+
+        hid_finish(0, got0)
+
+        hid2_p = sb("hid2_p", [P, 4, S], BF16)
+        for t in range(4):
+            gb = bank(4 + 2 * (t % 2))
+            eb = bank(5 + 2 * (t % 2))
+            cols = slice(P * t, P * (t + 1))
+            mm(gb[:], w3_q, cols, eq_w[:], eq_s[:])
+            mm(eb[:], w2_q, cols, eq_w[:], eq_s[:])
+            th = sb("th%d" % t, [P, S], F32)
+            nc.scalar.activation(th[:], gb[:], ACT.Tanh, scale=0.5)
+            gate = sb("gate%d" % t, [P, S], F32)
+            nc.scalar.activation(gate[:], th[:], ACT.Identity, scale=h2[:, t : t + 1], bias=h2[:, t : t + 1])
+            nc.vector.tensor_tensor(hid2_p[:, t, :], eb[:], gate[:], ALU.mult)
+        hid2_w = sb("hid2_w", [P, S, 4], BF16)
+        nc.vector.tensor_copy(hid2_w[:], hid2_p[:].rearrange("p t n -> p n t"))
+        hid2_c = sb("hid2_c", [P, S], U32)
+        hid2_s = sb("hid2_s", [P, S], U8)
+        nc.vector.quantize_mx(out=hid2_c[:].bitcast(FP8X4), scales=hid2_s[:], in_=hid2_w[:].rearrange("p n t -> p (n t)"))
+
+        bid_g = sb("bid_g", [P, S], F32)
+        nc.scalar.activation(bid_g[:], bid_tab[:].indirect(cmp_t[:]), ACT.Copy)
+
+        got1 = hid_gather(1)
+        hid_finish(1, got1)
+
+        vals = []
+        for b in range(4):
+            sc = bank(4 + b)
+            mm(sc[:], hid_q[b // 2], slice(P * (b % 2), P * (b % 2 + 1)), hid2_c[:], hid2_s[:])
+            tn = sb("tn%d" % b, [P, S], F32)
+            nc.scalar.activation(tn[:], sc[:], ACT.Tanh)
+            ex = sb("ex%d" % b, [P, S], F32)
+            nc.scalar.activation(ex[:], tn[:], ACT.Exp, scale=0.9)
+            val = sb("val%d" % b, [P, S], F32)
+            nc.vector.tensor_tensor(val[:], ex[:], bid_g[:], ALU.mult)
+            slot = sb("slot%d" % b, [P, P], F32)
+            val4 = val[:].rearrange("p (z d) -> p z d", d=4)
+            nc.vector.tensor_reduce(slot[:], val4, mybir.AxisListType.X, ALU.max)
+            lead = sb("lead%d" % b, [P, P, 4], F32)
+            nc.vector.tensor_tensor(lead[:], val4, slot[:].unsqueeze(2).to_broadcast([P, P, 4]), ALU.subtract)
+            vals.append((val, lead))
+            if b > 0:
+                finish(nc, sb, out, run_t, b - 1, vals[b - 1])
+        finish(nc, sb, out, run_t, 3, vals[3])
+
+
+def finish(nc, sb, out, run_t, b, pair):
+    val, lead = pair
+    damp = sb("damp%d" % b, [P, S], F32)
+    nc.scalar.activation(damp[:], lead[:].rearrange("p z d -> p (z d)"), ACT.Exp, scale=1.5)
+    res = sb("res%d" % b, [P, S], F32)
+    for h in range(2):
+        cols = slice(h * HALF, (h + 1) * HALF)
+        window = val[:].indirect(run_t[:, h * LH : (h + 1) * LH])
+        if b == 3:
+            nc.vector.tensor_tensor(res[:, cols], window, damp[:, cols], ALU.mult)
+        else:
+            picked = sb("picked%d_%d" % (b, h), [P, HALF], F32)
+            nc.scalar.activation(picked[:], window, ACT.Copy)
+            nc.vector.tensor_tensor(res[:, cols], picked[:], damp[:, cols], ALU.mult)
+    nc.sync.dma_start(out=out[P * b : P * (b + 1), :], in_=res[:])

@@ -31,8 +31,8 @@ def tile_picked_yauctbd_pay_p_kernel(
         keep = ctx.enter_context(tc.tile_pool(name="keep", bufs=1))
         psum = ctx.enter_context(tc.psum_pool(name="psum", bufs=1))
 
-        def sb(name, shape, dt):
-            return keep.tile(shape, dt, name=name, align_bytes=64)
+        def sb(name, shape, dt, tag=None):
+            return keep.tile(shape, dt, name=name, tag=tag or name, align_bytes=64)
 
         offs_t = keep.tile([P, S // 16], U16, name="offs_t")
         cmp_t = keep.tile([P, S // 16], U16, name="cmp_t")
@@ -47,9 +47,9 @@ def tile_picked_yauctbd_pay_p_kernel(
         rows = sb("rows", [P, P], F32)
         ident = sb("ident", [P, P], F32)
 
-        nc.vector.memset(xs_tab[:].bitcast(I32), 0)
-        nc.vector.memset(rows[:], 0.0)
-        nc.vector.memset(es_tab[:].bitcast(I32), 0)
+        nc.gpsimd.memset(xs_tab[:].bitcast(I32), 0)
+        nc.gpsimd.memset(rows[:], 0.0)
+        nc.gpsimd.memset(es_tab[:].bitcast(I32), 0)
         make_identity(nc, ident[:])
 
         def load_scales(eng, tab, scales):
@@ -103,9 +103,9 @@ def tile_picked_yauctbd_pay_p_kernel(
         nc.vector.tensor_scalar(sgn[:], ub[:, 0:4], 0.0, -0.5, ALU.is_ge, ALU.add)
         nc.vector.tensor_tensor(h2[:], sgn[:], ub[:, 4:8], ALU.mult)
 
-        def cast_half(eng, wb, raw, h):
-            dst = wb[:].rearrange("p (t h g r j) -> p h t g r j", t=4, h=2, g=8, r=8)[:, h]
-            srcv = raw[:].rearrange("p j (g t r) -> p t g r j", t=4, r=8)
+        def cast_half(eng, wb, raw, h, ts=slice(0, 4)):
+            dst = wb[:].rearrange("p (t h g r j) -> p h t g r j", t=4, h=2, g=8, r=8)[:, h, ts]
+            srcv = raw[:].rearrange("p j (g t r) -> p t g r j", t=4, r=8)[:, ts]
             if eng == "v":
                 nc.vector.tensor_copy(dst, srcv)
             else:
@@ -117,6 +117,17 @@ def tile_picked_yauctbd_pay_p_kernel(
             nc.vector.quantize_mx(out=codes[:].bitcast(FP8X4), scales=scales[:], in_=wb[:])
             return codes, scales
 
+        def last_half_and_quant(name, wb, raw):
+            codes = sb(name + "_c", [P, S], U32)
+            scales = sb(name + "_s", [P, S], U8)
+            for u in range(2):
+                cast_half("v", wb, raw, 1, slice(2 * u, 2 * u + 2))
+                cols = slice(u * HALF, (u + 1) * HALF)
+                nc.vector.quantize_mx(
+                    out=codes[:, cols].bitcast(FP8X4), scales=scales[:, cols], in_=wb[:, 4 * u * HALF : 4 * (u + 1) * HALF]
+                )
+            return codes, scales
+
         def mm(dst, lq, cols, rw, rs):
             nc.tensor.matmul_mx(
                 out=dst, lhsT=lq[0][:, cols].bitcast(FP8X4), lhsT_scale=lq[1][:, cols],
@@ -125,8 +136,7 @@ def tile_picked_yauctbd_pay_p_kernel(
 
         w1_b = sb("w1_b", [P, 4 * S], BF16)
         cast_half("s", w1_b, w1_raw[0], 0)
-        cast_half("v", w1_b, w1_raw[1], 1)
-        w1_q = quant("w1", w1_b)
+        w1_q = last_half_and_quant("w1", w1_b, w1_raw[1])
 
         y = []
         relu_y = []
@@ -151,31 +161,43 @@ def tile_picked_yauctbd_pay_p_kernel(
                 got.append(g)
             return got
 
-        def hid_finish(h, got):
-            planes = sb("hid_p%d" % h, [P, 4, HALF], BF16)
+        def weave(eng, name, planes):
+            woven = sb(name, [P, HALF, 4], BF16)
+            if eng == "v":
+                nc.vector.tensor_copy(woven[:], planes.rearrange("p t n -> p n t"))
+            else:
+                nc.scalar.copy(woven[:], planes.rearrange("p t n -> p n t"))
+            return woven
+
+        def quant_into(codes, scales, woven):
+            nc.vector.quantize_mx(out=codes.bitcast(FP8X4), scales=scales, in_=woven[:].rearrange("p n t -> p (n t)"))
+
+        def hid_sum(h, got, tag):
+            planes = sb("hid_p%d" % h, [P, 4, HALF], BF16, tag)
             for t in range(4):
                 nc.vector.scalar_tensor_tensor(
                     planes[:, t, :], y[t][:, h * HALF : (h + 1) * HALF], u_abs[:, t : t + 1], got[t][:], ALU.mult, ALU.add
                 )
-            woven = sb("hid_w%d" % h, [P, HALF, 4], BF16)
-            nc.vector.tensor_copy(woven[:], planes[:].rearrange("p t n -> p n t"))
+            return planes
+
+        def hid_quant(h, woven):
             codes = sb("hid_c%d" % h, [P, HALF], U32)
             scales = sb("hid_s%d" % h, [P, HALF], U8)
-            nc.vector.quantize_mx(out=codes[:].bitcast(FP8X4), scales=scales[:], in_=woven[:].rearrange("p n t -> p (n t)"))
+            quant_into(codes[:], scales[:], woven)
             hid_q.append((codes, scales))
 
         got0 = hid_gather(0)
+        got1 = hid_gather(1)
 
         w2_b = sb("w2_b", [P, 4 * S], BF16)
         w3_b = sb("w3_b", [P, 4 * S], BF16)
         cast_half("v", w2_b, w2_raw[0], 0)
         cast_half("v", w2_b, w2_raw[1], 1)
         w2_q = quant("w2", w2_b)
-        cast_half("s", w3_b, w3_raw[0], 0)
-        cast_half("v", w3_b, w3_raw[1], 1)
-        w3_q = quant("w3", w3_b)
+        cast_half("v", w3_b, w3_raw[0], 0)
+        w3_q = last_half_and_quant("w3", w3_b, w3_raw[1])
 
-        hid_finish(0, got0)
+        hid_p0 = hid_sum(0, got0, "w3_b")
 
         hid2_p = sb("hid2_p", [P, 4, S], BF16)
         for t in range(4):
@@ -187,53 +209,63 @@ def tile_picked_yauctbd_pay_p_kernel(
             th = sb("th%d" % t, [P, S], F32)
             nc.scalar.activation(th[:], gb[:], ACT.Tanh, scale=0.5)
             gate = sb("gate%d" % t, [P, S], F32)
-            nc.scalar.activation(gate[:], th[:], ACT.Identity, scale=h2[:, t : t + 1], bias=h2[:, t : t + 1])
+            nc.vector.tensor_scalar(gate[:], th[:], h2[:, t : t + 1], h2[:, t : t + 1], ALU.mult, ALU.add)
             nc.vector.tensor_tensor(hid2_p[:, t, :], eb[:], gate[:], ALU.mult)
-        hid2_w = sb("hid2_w", [P, S, 4], BF16)
-        nc.vector.tensor_copy(hid2_w[:], hid2_p[:].rearrange("p t n -> p n t"))
+
+        hid_w0 = weave("s", "hid_w0", hid_p0[:])
+        bid_g = sb("bid_g", [P, S], F32, "th2")
+        nc.scalar.activation(bid_g[:], bid_tab[:].indirect(cmp_t[:]), ACT.Copy)
         hid2_c = sb("hid2_c", [P, S], U32)
         hid2_s = sb("hid2_s", [P, S], U8)
-        nc.vector.quantize_mx(out=hid2_c[:].bitcast(FP8X4), scales=hid2_s[:], in_=hid2_w[:].rearrange("p n t -> p (n t)"))
+        hid2_w0 = weave("s", "hid2_w0", hid2_p[:, :, 0:HALF])
+        hid2_w1 = weave("v", "hid2_w1", hid2_p[:, :, HALF:S])
+        hid_quant(0, hid_w0)
+        quant_into(hid2_c[:, HALF:S], hid2_s[:, HALF:S], hid2_w1)
+        quant_into(hid2_c[:, 0:HALF], hid2_s[:, 0:HALF], hid2_w0)
 
-        bid_g = sb("bid_g", [P, S], F32)
-        nc.scalar.activation(bid_g[:], bid_tab[:].indirect(cmp_t[:]), ACT.Copy)
+        hid_p1 = hid_sum(1, got1, "hid2_w1")
+        hid_quant(1, weave("v", "hid_w1", hid_p1[:]))
 
-        got1 = hid_gather(1)
-        hid_finish(1, got1)
+        def tile_f32(name, b):
+            return sb("%s%d" % (name, b), [P, S], F32)
 
-        vals = []
-        for b in range(4):
+        def value(b):
             sc = bank(4 + b)
             mm(sc[:], hid_q[b // 2], slice(P * (b % 2), P * (b % 2 + 1)), hid2_c[:], hid2_s[:])
-            tn = sb("tn%d" % b, [P, S], F32)
+            tn = tile_f32("tn", b)
             nc.scalar.activation(tn[:], sc[:], ACT.Tanh)
-            ex = sb("ex%d" % b, [P, S], F32)
+            ex = tile_f32("ex", b)
             nc.scalar.activation(ex[:], tn[:], ACT.Exp, scale=0.9)
-            val = sb("val%d" % b, [P, S], F32)
+            val = tile_f32("val", b)
             nc.vector.tensor_tensor(val[:], ex[:], bid_g[:], ALU.mult)
+            return val
+
+        def lead_of(b, val):
+            picked = tile_f32("picked", b)
+            for h in range(2):
+                nc.scalar.activation(
+                    picked[:, h * HALF : (h + 1) * HALF], val[:].indirect(run_t[:, h * LH : (h + 1) * LH]), ACT.Copy
+                )
             slot = sb("slot%d" % b, [P, P], F32)
             val4 = val[:].rearrange("p (z d) -> p z d", d=4)
             nc.vector.tensor_reduce(slot[:], val4, mybir.AxisListType.X, ALU.max)
             lead = sb("lead%d" % b, [P, P, 4], F32)
             nc.vector.tensor_tensor(lead[:], val4, slot[:].unsqueeze(2).to_broadcast([P, P, 4]), ALU.subtract)
-            vals.append((val, lead))
-            if b > 0:
-                finish(nc, sb, out, run_t, b - 1, vals[b - 1])
-        finish(nc, sb, out, run_t, 3, vals[3])
+            return picked, lead
 
+        def finish(b, picked, lead):
+            damp = tile_f32("damp", b)
+            nc.scalar.activation(damp[:], lead[:].rearrange("p z d -> p (z d)"), ACT.Exp, scale=1.5)
+            res = tile_f32("res", b)
+            nc.vector.tensor_tensor(res[:], picked[:], damp[:], ALU.mult)
+            nc.sync.dma_start(out=out[P * b : P * (b + 1), :], in_=res[:])
 
-def finish(nc, sb, out, run_t, b, pair):
-    val, lead = pair
-    damp = sb("damp%d" % b, [P, S], F32)
-    nc.scalar.activation(damp[:], lead[:].rearrange("p z d -> p (z d)"), ACT.Exp, scale=1.5)
-    res = sb("res%d" % b, [P, S], F32)
-    for h in range(2):
-        cols = slice(h * HALF, (h + 1) * HALF)
-        window = val[:].indirect(run_t[:, h * LH : (h + 1) * LH])
-        if b == 3:
-            nc.vector.tensor_tensor(res[:, cols], window, damp[:, cols], ALU.mult)
-        else:
-            picked = sb("picked%d_%d" % (b, h), [P, HALF], F32)
-            nc.scalar.activation(picked[:], window, ACT.Copy)
-            nc.vector.tensor_tensor(res[:, cols], picked[:], damp[:, cols], ALU.mult)
-    nc.sync.dma_start(out=out[P * b : P * (b + 1), :], in_=res[:])
+        vals = {}
+        leads = {}
+        for step in range(6):
+            if step < 4:
+                vals[step] = value(step)
+            if 1 <= step < 5:
+                leads[step - 1] = lead_of(step - 1, vals[step - 1])
+            if step >= 2:
+                finish(step - 2, *leads[step - 2])

@@ -44,11 +44,12 @@ def tile_picked_yauctbd_pay_p_kernel(
         xs_tab = sb("xs_tab", [P, T], U8)
         es_tab = sb("es_tab", [P, W], U8)
         bid_tab = sb("bid_tab", [P, W], F32)
-        rows = sb("rows", [P, P], F32)
+        rows = [sb("rows%d" % a, [P, P], F32) for a in range(2)]
         ident = sb("ident", [P, P], F32)
 
         nc.gpsimd.memset(xs_tab[:].bitcast(I32), 0)
-        nc.gpsimd.memset(rows[:], 0.0)
+        nc.gpsimd.memset(rows[0][:], 0.0)
+        nc.gpsimd.memset(rows[1][:], 0.0)
         nc.gpsimd.memset(es_tab[:].bitcast(I32), 0)
         make_identity(nc, ident[:])
 
@@ -59,26 +60,29 @@ def tile_picked_yauctbd_pay_p_kernel(
         def load_words(tab, words):
             nc.sync.dma_start(out=tab[:], in_=words[0].rearrange("p n t -> p (n t)").bitcast(I32))
 
+        def load_factor(dst, vec):
+            nc.sync.dma_start(
+                out=dst[0:4, :].rearrange("t (g r) -> t g r", r=8), in_=vec.rearrange("(g t r) o -> t g (r o)", t=4, r=8)
+            )
+
         def load_half(name, w, h):
             raw = sb(name, [P, PACK, HALF], F32)
             nc.sync.dma_start(out=raw[:], in_=w.rearrange("(p j) c -> p j c", j=PACK)[:, :, h * HALF : (h + 1) * HALF])
             return raw
 
         nc.sync.dma_start(offs_t[:], offs)
-        load_words(x_tab, x_words)
+        w1_raw = [load_half("w1_raw0", w1, 0)]
         load_scales(nc.sync, xs_tab, x_scales)
-        for a, vec in enumerate((unit, unit2)):
-            nc.sync.dma_start(
-                out=rows[4 * a : 4 * a + 4, :].rearrange("t (g r) -> t g r", r=8),
-                in_=vec.rearrange("(g t r) o -> t g (r o)", t=4, r=8),
-            )
-        w1_raw = [load_half("w1_raw%d" % h, w1, h) for h in range(2)]
+        load_factor(rows[0], unit)
+        load_words(x_tab, x_words)
+        w1_raw.append(load_half("w1_raw1", w1, 1))
+        load_factor(rows[1], unit2)
         nc.sync.dma_start(cmp_t[:], cmp_)
         load_words(e_tab, e_words)
+        w3_raw = [load_half("w3_raw%d" % h, w3, h) for h in range(2)]
         load_scales(nc.sync, es_tab, e_scales)
         nc.sync.dma_start(usr_t[:], usr)
         w2_raw = [load_half("w2_raw%d" % h, w2, h) for h in range(2)]
-        w3_raw = [load_half("w3_raw%d" % h, w3, h) for h in range(2)]
         nc.sync.dma_start(out=bid_tab[:], in_=bid)
         nc.sync.dma_start(run_t[:], run)
 
@@ -86,22 +90,19 @@ def tile_picked_yauctbd_pay_p_kernel(
             return psum.tile([P, S], F32, name="bank%d" % i)
 
         xq_s = sb("xq_s", [P, S], U8)
-        eq_s = sb("eq_s", [P, S], U8)
-        xq_w = sb("xq_w", [P, S], U32)
-        eq_w = sb("eq_w", [P, S], U32)
-        nc.vector.tensor_copy(xq_w[:], x_tab[:].bitcast(U32).indirect(offs_t[:]))
-        nc.vector.tensor_copy(xq_s[:], xs_tab[:].indirect(offs_t[:]))
 
+
+        nc.vector.tensor_copy(xq_s[:], xs_tab[:].indirect(offs_t[:]))
         ub = bank(4)
-        nc.tensor.transpose(ub[:, 0:P], rows[:], ident[:])
+        nc.tensor.transpose(ub[:, 0:P], rows[0][:], ident[:])
         u_abs = sb("u_abs", [P, 4], F32)
         u_half = sb("u_half", [P, 4], F32)
         sgn = sb("sgn", [P, 4], F32)
-        h2 = sb("h2", [P, 4], F32)
         nc.scalar.activation(u_abs[:], ub[:, 0:4], ACT.Abs)
         nc.scalar.activation(u_half[:], ub[:, 0:4], ACT.Abs, scale=0.5)
         nc.vector.tensor_scalar(sgn[:], ub[:, 0:4], 0.0, -0.5, ALU.is_ge, ALU.add)
-        nc.vector.tensor_tensor(h2[:], sgn[:], ub[:, 4:8], ALU.mult)
+        xq_w = sb("xq_w", [P, S], U32)
+        nc.vector.tensor_copy(xq_w[:], x_tab[:].bitcast(U32).indirect(offs_t[:]))
 
         def cast_half(eng, wb, raw, h, ts=slice(0, 4)):
             dst = wb[:].rearrange("p (t h g r j) -> p h t g r j", t=4, h=2, g=8, r=8)[:, h, ts]
@@ -117,11 +118,11 @@ def tile_picked_yauctbd_pay_p_kernel(
             nc.vector.quantize_mx(out=codes[:].bitcast(FP8X4), scales=scales[:], in_=wb[:])
             return codes, scales
 
-        def last_half_and_quant(name, wb, raw):
+        def last_half_and_quant(name, wb, raw, engines):
             codes = sb(name + "_c", [P, S], U32)
             scales = sb(name + "_s", [P, S], U8)
             for u in range(2):
-                cast_half("v", wb, raw, 1, slice(2 * u, 2 * u + 2))
+                cast_half(engines[u], wb, raw, 1, slice(2 * u, 2 * u + 2))
                 cols = slice(u * HALF, (u + 1) * HALF)
                 nc.vector.quantize_mx(
                     out=codes[:, cols].bitcast(FP8X4), scales=scales[:, cols], in_=wb[:, 4 * u * HALF : 4 * (u + 1) * HALF]
@@ -136,7 +137,7 @@ def tile_picked_yauctbd_pay_p_kernel(
 
         w1_b = sb("w1_b", [P, 4 * S], BF16)
         cast_half("s", w1_b, w1_raw[0], 0)
-        w1_q = last_half_and_quant("w1", w1_b, w1_raw[1])
+        w1_q = last_half_and_quant("w1", w1_b, w1_raw[1], "vs")
 
         y = []
         relu_y = []
@@ -148,21 +149,23 @@ def tile_picked_yauctbd_pay_p_kernel(
             y.append(yb)
             relu_y.append(r)
 
-        nc.vector.tensor_copy(eq_s[:], es_tab[:].indirect(cmp_t[:]))
+        ub2 = bank(5)
+        nc.tensor.transpose(ub2[:, 0:P], rows[1][:], ident[:])
+        h2 = sb("h2", [P, 4], F32)
+        nc.vector.tensor_tensor(h2[:], sgn[:], ub2[:, 0:4], ALU.mult)
+        eq_w = sb("eq_w", [P, S], U32, "w1_b")
         nc.vector.tensor_copy(eq_w[:], e_tab[:].bitcast(U32).indirect(cmp_t[:]))
 
         hid_q = []
 
-        def hid_gather(h):
-            got = []
+        def hid_gather(h, tag):
+            got = sb("ru%d" % h, [P, 4, HALF], F32, tag)
             for t in range(4):
-                g = sb("ru%d_%d" % (h, t), [P, HALF], F32)
-                nc.scalar.activation(g[:], relu_y[t][:].indirect(usr_t[:, h * LH : (h + 1) * LH]), ACT.Copy)
-                got.append(g)
+                nc.scalar.activation(got[:, t, :], relu_y[t][:].indirect(usr_t[:, h * LH : (h + 1) * LH]), ACT.Copy)
             return got
 
-        def weave(eng, name, planes):
-            woven = sb(name, [P, HALF, 4], BF16)
+        def weave(eng, name, planes, width=HALF):
+            woven = sb(name, [P, width, 4], BF16)
             if eng == "v":
                 nc.vector.tensor_copy(woven[:], planes.rearrange("p t n -> p n t"))
             else:
@@ -176,7 +179,7 @@ def tile_picked_yauctbd_pay_p_kernel(
             planes = sb("hid_p%d" % h, [P, 4, HALF], BF16, tag)
             for t in range(4):
                 nc.vector.scalar_tensor_tensor(
-                    planes[:, t, :], y[t][:, h * HALF : (h + 1) * HALF], u_abs[:, t : t + 1], got[t][:], ALU.mult, ALU.add
+                    planes[:, t, :], y[t][:, h * HALF : (h + 1) * HALF], u_abs[:, t : t + 1], got[:, t, :], ALU.mult, ALU.add
                 )
             return planes
 
@@ -186,44 +189,48 @@ def tile_picked_yauctbd_pay_p_kernel(
             quant_into(codes[:], scales[:], woven)
             hid_q.append((codes, scales))
 
-        got0 = hid_gather(0)
-        got1 = hid_gather(1)
-
-        w2_b = sb("w2_b", [P, 4 * S], BF16)
-        w3_b = sb("w3_b", [P, 4 * S], BF16)
-        cast_half("v", w2_b, w2_raw[0], 0)
-        cast_half("v", w2_b, w2_raw[1], 1)
-        w2_q = quant("w2", w2_b)
+        w3_b = sb("w3_b", [P, 4 * S], BF16, "e_tab")
         cast_half("v", w3_b, w3_raw[0], 0)
-        w3_q = last_half_and_quant("w3", w3_b, w3_raw[1])
+        cast_half("v", w3_b, w3_raw[1], 1)
+        w3_q = quant("w3", w3_b)
+        eq_s = sb("eq_s", [P, S], U8, "e_tab")
+        nc.vector.tensor_copy(eq_s[:], es_tab[:].indirect(cmp_t[:]))
 
-        hid_p0 = hid_sum(0, got0, "w3_b")
+        got0 = hid_gather(0, None)
 
-        hid2_p = sb("hid2_p", [P, 4, S], BF16)
+        gates = []
         for t in range(4):
-            gb = bank(4 + 2 * (t % 2))
-            eb = bank(5 + 2 * (t % 2))
-            cols = slice(P * t, P * (t + 1))
-            mm(gb[:], w3_q, cols, eq_w[:], eq_s[:])
-            mm(eb[:], w2_q, cols, eq_w[:], eq_s[:])
+            gb = bank(4 + t)
+            mm(gb[:], w3_q, slice(P * t, P * (t + 1)), eq_w[:], eq_s[:])
             th = sb("th%d" % t, [P, S], F32)
             nc.scalar.activation(th[:], gb[:], ACT.Tanh, scale=0.5)
             gate = sb("gate%d" % t, [P, S], F32)
-            nc.vector.tensor_scalar(gate[:], th[:], h2[:, t : t + 1], h2[:, t : t + 1], ALU.mult, ALU.add)
-            nc.vector.tensor_tensor(hid2_p[:, t, :], eb[:], gate[:], ALU.mult)
+            nc.gpsimd.tensor_scalar(gate[:], th[:], h2[:, t : t + 1], h2[:, t : t + 1], ALU.mult, ALU.add)
+            gates.append(gate)
+
+        w2_b = sb("w2_b", [P, 4 * S], BF16, "es_tab")
+        cast_half("v", w2_b, w2_raw[0], 0)
+        w2_q = last_half_and_quant("w2", w2_b, w2_raw[1], "vv")
+
+        hid_p0 = hid_sum(0, got0, "es_tab")
+
+        hid2_p = sb("hid2_p", [P, 4, S], BF16)
+        for t in range(4):
+            eb = bank(4 + t)
+            mm(eb[:], w2_q, slice(P * t, P * (t + 1)), eq_w[:], eq_s[:])
+            nc.vector.tensor_tensor(hid2_p[:, t, :], eb[:], gates[t][:], ALU.mult)
 
         hid_w0 = weave("s", "hid_w0", hid_p0[:])
         bid_g = sb("bid_g", [P, S], F32, "th2")
         nc.scalar.activation(bid_g[:], bid_tab[:].indirect(cmp_t[:]), ACT.Copy)
         hid2_c = sb("hid2_c", [P, S], U32)
         hid2_s = sb("hid2_s", [P, S], U8)
-        hid2_w0 = weave("s", "hid2_w0", hid2_p[:, :, 0:HALF])
-        hid2_w1 = weave("v", "hid2_w1", hid2_p[:, :, HALF:S])
+        hid2_w = weave("v", "hid2_w", hid2_p[:], S)
         hid_quant(0, hid_w0)
-        quant_into(hid2_c[:, HALF:S], hid2_s[:, HALF:S], hid2_w1)
-        quant_into(hid2_c[:, 0:HALF], hid2_s[:, 0:HALF], hid2_w0)
+        quant_into(hid2_c[:], hid2_s[:], hid2_w)
 
-        hid_p1 = hid_sum(1, got1, "hid2_w1")
+        got1 = hid_gather(1, "es_tab")
+        hid_p1 = hid_sum(1, got1, "hid2_w")
         hid_quant(1, weave("v", "hid_w1", hid_p1[:]))
 
         def tile_f32(name, b):
@@ -243,9 +250,11 @@ def tile_picked_yauctbd_pay_p_kernel(
         def lead_of(b, val):
             picked = tile_f32("picked", b)
             for h in range(2):
-                nc.scalar.activation(
-                    picked[:, h * HALF : (h + 1) * HALF], val[:].indirect(run_t[:, h * LH : (h + 1) * LH]), ACT.Copy
-                )
+                window = val[:].indirect(run_t[:, h * LH : (h + 1) * LH])
+                if b == 0:
+                    nc.vector.tensor_copy(picked[:, h * HALF : (h + 1) * HALF], window)
+                else:
+                    nc.scalar.activation(picked[:, h * HALF : (h + 1) * HALF], window, ACT.Copy)
             slot = sb("slot%d" % b, [P, P], F32)
             val4 = val[:].rearrange("p (z d) -> p z d", d=4)
             nc.vector.tensor_reduce(slot[:], val4, mybir.AxisListType.X, ALU.max)
@@ -255,10 +264,13 @@ def tile_picked_yauctbd_pay_p_kernel(
 
         def finish(b, picked, lead):
             damp = tile_f32("damp", b)
-            nc.scalar.activation(damp[:], lead[:].rearrange("p z d -> p (z d)"), ACT.Exp, scale=1.5)
             res = tile_f32("res", b)
-            nc.vector.tensor_tensor(res[:], picked[:], damp[:], ALU.mult)
-            nc.sync.dma_start(out=out[P * b : P * (b + 1), :], in_=res[:])
+            width = HALF if b == 3 else S
+            for c in range(0, S, width):
+                cols = slice(c, c + width)
+                nc.scalar.activation(damp[:, cols], lead[:].rearrange("p z d -> p (z d)")[:, cols], ACT.Exp, scale=1.5)
+                nc.vector.tensor_tensor(res[:, cols], picked[:, cols], damp[:, cols], ALU.mult)
+                nc.sync.dma_start(out=out[P * b : P * (b + 1), cols], in_=res[:, cols])
 
         vals = {}
         leads = {}

@@ -62,7 +62,7 @@ def tile_picked_yauctbd_pay_p_kernel(
 
         def load_factor(dst, vec):
             nc.sync.dma_start(
-                out=dst[0:4, :].rearrange("t (g r) -> t g r", r=8), in_=vec.rearrange("(g t r) o -> t g (r o)", t=4, r=8)
+                out=dst[0:4, :].rearrange("t (g i) -> t g i", i=4), in_=vec.rearrange("(g t i) o -> t g (i o)", t=4, i=4)
             )
 
         def load_half(name, w, h):
@@ -105,8 +105,8 @@ def tile_picked_yauctbd_pay_p_kernel(
         nc.vector.tensor_copy(xq_w[:], x_tab[:].bitcast(U32).indirect(offs_t[:]))
 
         def cast_half(eng, wb, raw, h, ts=slice(0, 4)):
-            dst = wb[:].rearrange("p (t h g r j) -> p h t g r j", t=4, h=2, g=8, r=8)[:, h, ts]
-            srcv = raw[:].rearrange("p j (g t r) -> p t g r j", t=4, r=8)[:, ts]
+            dst = wb[:].rearrange("p (t h g i j) -> p h t g j i", t=4, h=2, g=16, i=4)[:, h, ts]
+            srcv = raw[:].rearrange("p j (g t i) -> p t g j i", t=4, i=4)[:, ts]
             if eng == "v":
                 nc.vector.tensor_copy(dst, srcv)
             else:
@@ -152,7 +152,9 @@ def tile_picked_yauctbd_pay_p_kernel(
         ub2 = bank(5)
         nc.tensor.transpose(ub2[:, 0:P], rows[1][:], ident[:])
         h2 = sb("h2", [P, 4], F32)
-        nc.vector.tensor_tensor(h2[:], sgn[:], ub2[:, 0:4], ALU.mult)
+        u2 = sb("u2", [P, 4], F32)
+        nc.scalar.copy(u2[:], ub2[:, 0:4])
+        nc.gpsimd.tensor_tensor(h2[:], sgn[:], u2[:], ALU.mult)
         eq_w = sb("eq_w", [P, S], U32, "w1_b")
         nc.vector.tensor_copy(eq_w[:], e_tab[:].bitcast(U32).indirect(cmp_t[:]))
 
@@ -166,10 +168,12 @@ def tile_picked_yauctbd_pay_p_kernel(
 
         def weave(eng, name, planes, width=HALF):
             woven = sb(name, [P, width, 4], BF16)
+            dst = woven[:].rearrange("p (c i) t -> p c t i", i=4)
+            srcv = planes.rearrange("p t (c i) -> p c t i", i=4)
             if eng == "v":
-                nc.vector.tensor_copy(woven[:], planes.rearrange("p t n -> p n t"))
+                nc.vector.tensor_copy(dst, srcv)
             else:
-                nc.scalar.copy(woven[:], planes.rearrange("p t n -> p n t"))
+                nc.scalar.copy(dst, srcv)
             return woven
 
         def quant_into(codes, scales, woven):
@@ -210,7 +214,8 @@ def tile_picked_yauctbd_pay_p_kernel(
 
         w2_b = sb("w2_b", [P, 4 * S], BF16, "es_tab")
         cast_half("v", w2_b, w2_raw[0], 0)
-        w2_q = last_half_and_quant("w2", w2_b, w2_raw[1], "vv")
+        cast_half("v", w2_b, w2_raw[1], 1)
+        w2_q = quant("w2", w2_b)
 
         hid_p0 = hid_sum(0, got0, "es_tab")
 
@@ -221,7 +226,7 @@ def tile_picked_yauctbd_pay_p_kernel(
             nc.vector.tensor_tensor(hid2_p[:, t, :], eb[:], gates[t][:], ALU.mult)
 
         hid_w0 = weave("s", "hid_w0", hid_p0[:])
-        bid_g = sb("bid_g", [P, S], F32, "th2")
+        bid_g = sb("bid_g", [P, S], F32, "th0")
         nc.scalar.activation(bid_g[:], bid_tab[:].indirect(cmp_t[:]), ACT.Copy)
         hid2_c = sb("hid2_c", [P, S], U32)
         hid2_s = sb("hid2_s", [P, S], U8)

@@ -62,7 +62,7 @@ def tile_picked_yauctbd_pay_p_kernel(
 
         def load_factor(dst, vec):
             nc.sync.dma_start(
-                out=dst[0:4, :].rearrange("t (g i) -> t g i", i=4), in_=vec.rearrange("(g t i) o -> t g (i o)", t=4, i=4)
+                out=dst[0:4, :].rearrange("t (g r) -> t g r", r=8), in_=vec.rearrange("(g t r) o -> t g (r o)", t=4, r=8)
             )
 
         def load_half(name, w, h):
@@ -105,8 +105,8 @@ def tile_picked_yauctbd_pay_p_kernel(
         nc.vector.tensor_copy(xq_w[:], x_tab[:].bitcast(U32).indirect(offs_t[:]))
 
         def cast_half(eng, wb, raw, h, ts=slice(0, 4)):
-            dst = wb[:].rearrange("p (t h g i j) -> p h t g j i", t=4, h=2, g=16, i=4)[:, h, ts]
-            srcv = raw[:].rearrange("p j (g t i) -> p t g j i", t=4, i=4)[:, ts]
+            dst = wb[:].rearrange("p (t h g r j) -> p h t g r j", t=4, h=2, g=8, r=8)[:, h, ts]
+            srcv = raw[:].rearrange("p j (g t r) -> p t g r j", t=4, r=8)[:, ts]
             if eng == "v":
                 nc.vector.tensor_copy(dst, srcv)
             else:
@@ -168,8 +168,8 @@ def tile_picked_yauctbd_pay_p_kernel(
 
         def weave(eng, name, planes, width=HALF):
             woven = sb(name, [P, width, 4], BF16)
-            dst = woven[:].rearrange("p (c i) t -> p c t i", i=4)
-            srcv = planes.rearrange("p t (c i) -> p c t i", i=4)
+            dst = woven[:]
+            srcv = planes.rearrange("p t n -> p n t")
             if eng == "v":
                 nc.vector.tensor_copy(dst, srcv)
             else:
@@ -253,12 +253,11 @@ def tile_picked_yauctbd_pay_p_kernel(
             return val
 
         def lead_of(b, val):
-            picked = tile_f32("picked", b)
-            for h in range(2):
-                window = val[:].indirect(run_t[:, h * LH : (h + 1) * LH])
-                if b == 0:
-                    nc.vector.tensor_copy(picked[:, h * HALF : (h + 1) * HALF], window)
-                else:
+            picked = None
+            if b > 0:
+                picked = tile_f32("picked", b)
+                for h in range(2):
+                    window = val[:].indirect(run_t[:, h * LH : (h + 1) * LH])
                     nc.scalar.activation(picked[:, h * HALF : (h + 1) * HALF], window, ACT.Copy)
             slot = sb("slot%d" % b, [P, P], F32)
             val4 = val[:].rearrange("p (z d) -> p z d", d=4)
@@ -274,7 +273,13 @@ def tile_picked_yauctbd_pay_p_kernel(
             for c in range(0, S, width):
                 cols = slice(c, c + width)
                 nc.scalar.activation(damp[:, cols], lead[:].rearrange("p z d -> p (z d)")[:, cols], ACT.Exp, scale=1.5)
-                nc.vector.tensor_tensor(res[:, cols], picked[:, cols], damp[:, cols], ALU.mult)
+                if b > 0:
+                    nc.vector.tensor_tensor(res[:, cols], picked[:, cols], damp[:, cols], ALU.mult)
+                else:
+                    for h in range(2):
+                        part = slice(h * HALF, (h + 1) * HALF)
+                        window = vals[b][:].indirect(run_t[:, h * LH : (h + 1) * LH])
+                        nc.vector.tensor_tensor(res[:, part], window, damp[:, part], ALU.mult)
                 nc.sync.dma_start(out=out[P * b : P * (b + 1), cols], in_=res[:, cols])
 
         vals = {}

from contextlib import ExitStack

import concourse.mybir as mybir
from concourse.masks import make_identity

K, T, W = 512, 2048, 1024
S = 512
FLOPS = 4 * 2 * 512 * 512 * 512

F32 = mybir.dt.float32
BF16 = mybir.dt.bfloat16
I32 = mybir.dt.int32
U32 = mybir.dt.uint32
U16 = mybir.dt.uint16
U8 = mybir.dt.uint8
FP8X4 = mybir.dt.float8_e4m3fn_x4
ALU = mybir.AluOpType
ACT = mybir.ActivationFunctionType

P = 128
PACK = 4
HALF = 256
LH = HALF // 16


def tile_picked_yauctbd_pay_p_kernel(
    tc, x_words, x_scales, w1, e_words, e_scales, w2, w3, unit, unit2, bid, offs, cmp_, usr, run, out
):
    nc = tc.nc
    with ExitStack() as ctx:
        keep = ctx.enter_context(tc.tile_pool(name="keep", bufs=1))
        psum = ctx.enter_context(tc.psum_pool(name="psum", bufs=1))

        def sb(name, shape, dt, tag=None):
            return keep.tile(shape, dt, name=name, tag=tag or name, align_bytes=64)

        offs_t = keep.tile([P, S // 16], U16, name="offs_t")
        cmp_t = keep.tile([P, S // 16], U16, name="cmp_t")
        usr_t = keep.tile([P, S // 16], U16, name="usr_t")
        run_t = keep.tile([P, S // 16], U16, name="run_t")

        x_tab = sb("x_tab", [P, T], I32)
        e_tab = sb("e_tab", [P, W], I32)
        xs_tab = sb("xs_tab", [P, T], U8)
        es_tab = sb("es_tab", [P, W], U8)
        bid_tab = sb("bid_tab", [P, W], F32)
        rows = [sb("rows%d" % a, [P, P], F32) for a in range(2)]
        ident = sb("ident", [P, P], F32)

        nc.gpsimd.memset(xs_tab[:].bitcast(I32), 0)
        nc.gpsimd.memset(rows[0][:], 0.0)
        nc.gpsimd.memset(rows[1][:], 0.0)
        nc.gpsimd.memset(es_tab[:].bitcast(I32), 0)
        make_identity(nc, ident[:])

        def load_scales(eng, tab, scales):
            for q in range(4):
                eng.dma_start(out=tab[32 * q : 32 * q + 4, :].bitcast(I32), in_=scales[0, 4 * q : 4 * q + 4, :].bitcast(I32))

        def load_words(tab, words):
            nc.sync.dma_start(out=tab[:], in_=words[0].rearrange("p n t -> p (n t)").bitcast(I32))

        def load_factor(dst, vec):
            nc.sync.dma_start(
                out=dst[0:4, :].rearrange("t (g r) -> t g r", r=8), in_=vec.rearrange("(g t r) o -> t g (r o)", t=4, r=8)
            )

        def load_half(name, w, h):
            raw = sb(name, [P, PACK, HALF], F32)
            nc.sync.dma_start(out=raw[:], in_=w.rearrange("(p j) c -> p j c", j=PACK)[:, :, h * HALF : (h + 1) * HALF])
            return raw

        nc.sync.dma_start(offs_t[:], offs)
        w1_raw = [load_half("w1_raw0", w1, 0)]
        load_scales(nc.sync, xs_tab, x_scales)
        load_factor(rows[0], unit)
        load_words(x_tab, x_words)
        w1_raw.append(load_half("w1_raw1", w1, 1))
        load_factor(rows[1], unit2)
        nc.sync.dma_start(cmp_t[:], cmp_)
        load_words(e_tab, e_words)
        w3_raw = [load_half("w3_raw%d" % h, w3, h) for h in range(2)]
        load_scales(nc.sync, es_tab, e_scales)
        nc.sync.dma_start(usr_t[:], usr)
        w2_raw = [load_half("w2_raw%d" % h, w2, h) for h in range(2)]
        nc.sync.dma_start(out=bid_tab[:], in_=bid)
        nc.sync.dma_start(run_t[:], run)

        def bank(i):
            return psum.tile([P, S], F32, name="bank%d" % i)

        xq_s = sb("xq_s", [P, S], U8)


        nc.vector.tensor_copy(xq_s[:], xs_tab[:].indirect(offs_t[:]))
        ub = bank(4)
        nc.tensor.transpose(ub[:, 0:P], rows[0][:], ident[:])
        u_abs = sb("u_abs", [P, 4], F32)
        u_half = sb("u_half", [P, 4], F32)
        sgn = sb("sgn", [P, 4], F32)
        nc.scalar.activation(u_abs[:], ub[:, 0:4], ACT.Abs)
        nc.scalar.activation(u_half[:], ub[:, 0:4], ACT.Abs, scale=0.5)
        nc.vector.tensor_scalar(sgn[:], ub[:, 0:4], 0.0, -0.5, ALU.is_ge, ALU.add)
        xq_w = sb("xq_w", [P, S], U32)
        nc.vector.tensor_copy(xq_w[:], x_tab[:].bitcast(U32).indirect(offs_t[:]))

        def cast_half(eng, wb, raw, h, ts=slice(0, 4)):
            dst = wb[:].rearrange("p (t h g r j) -> p h t g r j", t=4, h=2, g=8, r=8)[:, h, ts]
            srcv = raw[:].rearrange("p j (g t r) -> p t g r j", t=4, r=8)[:, ts]
            if eng == "v":
                nc.vector.tensor_copy(dst, srcv)
            else:
                nc.scalar.copy(dst, srcv)

        def quant(name, wb):
            codes = sb(name + "_c", [P, S], U32)
            scales = sb(name + "_s", [P, S], U8)
            nc.vector.quantize_mx(out=codes[:].bitcast(FP8X4), scales=scales[:], in_=wb[:])
            return codes, scales

        def last_half_and_quant(name, wb, raw, engines):
            codes = sb(name + "_c", [P, S], U32)
            scales = sb(name + "_s", [P, S], U8)
            for u in range(2):
                cast_half(engines[u], wb, raw, 1, slice(2 * u, 2 * u + 2))
                cols = slice(u * HALF, (u + 1) * HALF)
                nc.vector.quantize_mx(
                    out=codes[:, cols].bitcast(FP8X4), scales=scales[:, cols], in_=wb[:, 4 * u * HALF : 4 * (u + 1) * HALF]
                )
            return codes, scales

        def mm(dst, lq, cols, rw, rs):
            nc.tensor.matmul_mx(
                out=dst, lhsT=lq[0][:, cols].bitcast(FP8X4), lhsT_scale=lq[1][:, cols],
                rhs=rw.bitcast(FP8X4), rhs_scale=rs, start=True, stop=True,
            )

        w1_b = sb("w1_b", [P, 4 * S], BF16)
        cast_half("s", w1_b, w1_raw[0], 0)
        w1_q = last_half_and_quant("w1", w1_b, w1_raw[1], "vs")

        y = []
        relu_y = []
        for t in range(4):
            yb = bank(t)
            mm(yb[:], w1_q, slice(P * t, P * (t + 1)), xq_w[:], xq_s[:])
            r = sb("relu_y%d" % t, [P, S], F32)
            nc.scalar.activation(r[:], yb[:], ACT.Relu, scale=u_half[:, t : t + 1])
            y.append(yb)
            relu_y.append(r)

        ub2 = bank(5)
        nc.tensor.transpose(ub2[:, 0:P], rows[1][:], ident[:])
        h2 = sb("h2", [P, 4], F32)
        u2 = sb("u2", [P, 4], F32)
        nc.scalar.copy(u2[:], ub2[:, 0:4])
        nc.gpsimd.tensor_tensor(h2[:], sgn[:], u2[:], ALU.mult)
        eq_w = sb("eq_w", [P, S], U32, "w1_b")
        nc.vector.tensor_copy(eq_w[:], e_tab[:].bitcast(U32).indirect(cmp_t[:]))

        hid_q = []

        def hid_gather(h, tag):
            got = sb("ru%d" % h, [P, 4, HALF], F32, tag)
            for t in range(4):
                nc.scalar.activation(got[:, t, :], relu_y[t][:].indirect(usr_t[:, h * LH : (h + 1) * LH]), ACT.Copy)
            return got

        def weave(eng, name, planes, width=HALF):
            woven = sb(name, [P, width, 4], BF16)
            dst = woven[:]
            srcv = planes.rearrange("p t n -> p n t")
            if eng == "v":
                nc.vector.tensor_copy(dst, srcv)
            else:
                nc.scalar.copy(dst, srcv)
            return woven

        def quant_into(codes, scales, woven):
            nc.vector.quantize_mx(out=codes.bitcast(FP8X4), scales=scales, in_=woven[:].rearrange("p n t -> p (n t)"))

        def hid_sum(h, got, tag):
            planes = sb("hid_p%d" % h, [P, 4, HALF], BF16, tag)
            for t in range(4):
                nc.vector.scalar_tensor_tensor(
                    planes[:, t, :], y[t][:, h * HALF : (h + 1) * HALF], u_abs[:, t : t + 1], got[:, t, :], ALU.mult, ALU.add
                )
            return planes

        def hid_quant(h, woven):
            codes = sb("hid_c%d" % h, [P, HALF], U32)
            scales = sb("hid_s%d" % h, [P, HALF], U8)
            quant_into(codes[:], scales[:], woven)
            hid_q.append((codes, scales))

        w3_b = sb("w3_b", [P, 4 * S], BF16, "e_tab")
        cast_half("v", w3_b, w3_raw[0], 0)
        cast_half("v", w3_b, w3_raw[1], 1)
        w3_q = quant("w3", w3_b)
        eq_s = sb("eq_s", [P, S], U8, "e_tab")
        nc.vector.tensor_copy(eq_s[:], es_tab[:].indirect(cmp_t[:]))

        got0 = hid_gather(0, None)

        gates = []
        for t in range(4):
            gb = bank(4 + t)
            mm(gb[:], w3_q, slice(P * t, P * (t + 1)), eq_w[:], eq_s[:])
            th = sb("th%d" % t, [P, S], F32)
            nc.scalar.activation(th[:], gb[:], ACT.Tanh, scale=0.5)
            gate = sb("gate%d" % t, [P, S], F32)
            nc.gpsimd.tensor_scalar(gate[:], th[:], h2[:, t : t + 1], h2[:, t : t + 1], ALU.mult, ALU.add)
            gates.append(gate)

        w2_b = sb("w2_b", [P, 4 * S], BF16, "es_tab")
        cast_half("v", w2_b, w2_raw[0], 0)
        cast_half("v", w2_b, w2_raw[1], 1)
        w2_q = quant("w2", w2_b)

        hid_p0 = hid_sum(0, got0, "es_tab")

        hid2_p = sb("hid2_p", [P, 4, S], BF16)
        for t in range(4):
            eb = bank(4 + t)
            mm(eb[:], w2_q, slice(P * t, P * (t + 1)), eq_w[:], eq_s[:])
            nc.vector.tensor_tensor(hid2_p[:, t, :], eb[:], gates[t][:], ALU.mult)

        hid_w0 = weave("s", "hid_w0", hid_p0[:])
        bid_g = sb("bid_g", [P, S], F32, "th0")
        nc.scalar.activation(bid_g[:], bid_tab[:].indirect(cmp_t[:]), ACT.Copy)
        hid2_c = sb("hid2_c", [P, S], U32)
        hid2_s = sb("hid2_s", [P, S], U8)
        hid2_w = weave("v", "hid2_w", hid2_p[:], S)
        hid_quant(0, hid_w0)
        quant_into(hid2_c[:], hid2_s[:], hid2_w)

        got1 = hid_gather(1, "es_tab")
        hid_p1 = hid_sum(1, got1, "hid2_w")
        hid_quant(1, weave("v", "hid_w1", hid_p1[:]))

        def tile_f32(name, b):
            return sb("%s%d" % (name, b), [P, S], F32)

        def value(b):
            sc = bank(4 + b)
            mm(sc[:], hid_q[b // 2], slice(P * (b % 2), P * (b % 2 + 1)), hid2_c[:], hid2_s[:])
            tn = tile_f32("tn", b)
            nc.scalar.activation(tn[:], sc[:], ACT.Tanh)
            ex = tile_f32("ex", b)
            nc.scalar.activation(ex[:], tn[:], ACT.Exp, scale=0.9)
            val = tile_f32("val", b)
            nc.vector.tensor_tensor(val[:], ex[:], bid_g[:], ALU.mult)
            return val

        def lead_of(b, val):
            picked = None
            if b > 0:
                picked = tile_f32("picked", b)
                for h in range(2):
                    window = val[:].indirect(run_t[:, h * LH : (h + 1) * LH])
                    nc.scalar.activation(picked[:, h * HALF : (h + 1) * HALF], window, ACT.Copy)
            slot = sb("slot%d" % b, [P, P], F32)
            val4 = val[:].rearrange("p (z d) -> p z d", d=4)
            nc.vector.tensor_reduce(slot[:], val4, mybir.AxisListType.X, ALU.max)
            lead = sb("lead%d" % b, [P, P, 4], F32)
            nc.vector.tensor_tensor(lead[:], val4, slot[:].unsqueeze(2).to_broadcast([P, P, 4]), ALU.subtract)
            return picked, lead

        def finish(b, picked, lead):
            damp = tile_f32("damp", b)
            res = tile_f32("res", b)
            width = HALF if b == 3 else S
            for c in range(0, S, width):
                cols = slice(c, c + width)
                nc.scalar.activation(damp[:, cols], lead[:].rearrange("p z d -> p (z d)")[:, cols], ACT.Exp, scale=1.5)
                if b > 0:
                    nc.vector.tensor_tensor(res[:, cols], picked[:, cols], damp[:, cols], ALU.mult)
                else:
                    for h in range(2):
                        part = slice(h * HALF, (h + 1) * HALF)
                        window = vals[b][:].indirect(run_t[:, h * LH : (h + 1) * LH])
                        nc.vector.tensor_tensor(res[:, part], window, damp[:, part], ALU.mult)
                nc.sync.dma_start(out=out[P * b : P * (b + 1), cols], in_=res[:, cols])

        vals = {}
        leads = {}
        for step in range(6):
            if step < 4:
                vals[step] = value(step)
            if 1 <= step < 5:
                leads[step - 1] = lead_of(step - 1, vals[step - 1])
            if step >= 2:
                finish(step - 2, *leads[step - 2])
